import numpy as np
import ml_dtypes


def mxq(x, axis, fmt="e4m3"):
    dtype, down = {"e4m3": (ml_dtypes.float8_e4m3fn, 7), "e5m2": (ml_dtypes.float8_e5m2, 14)}[fmt]
    v = np.moveaxis(np.asarray(x, np.float32).astype(ml_dtypes.bfloat16).astype(np.float64), axis, -1)
    blocks = v.reshape(v.shape[:-1] + (-1, 32))
    amax = np.abs(blocks).max(-1, keepdims=True)
    byte = np.maximum(np.where(amax > 0, np.frexp(amax)[1] - 1 + 127, 0) - down, 1)
    scale = np.exp2(byte - 127.0)
    codes = (blocks / scale).astype(np.float32).astype(dtype).astype(np.float64)
    return np.moveaxis((codes * scale).reshape(v.shape), -1, axis)


WIDE = False


def mx_kscale(k):
    if not WIDE:
        return np.ones(k)
    levels = np.array([10, -10, 5, -5, 0])
    if k % 512:
        return np.exp2(np.random.permutation(np.resize(levels, k // 32))).repeat(32)
    a = np.empty((k // 512, 16))
    for p in range(k // 512):
        a[p, :8] = np.random.permutation(np.resize(levels, 8))
        for g in range(8):
            far = levels[np.abs(levels - a[p, g]) >= 10]
            a[p, g + 8] = far[np.random.randint(len(far))]
    return np.exp2(a.ravel()).repeat(32)


def f64(x):
    return np.asarray(x).astype(np.float64)


def striped(idx):
    return np.tile(idx.reshape(-1, 16).T, (8, 1)).astype(np.uint16)


def unstriped(offs):
    return offs[:16].T.reshape(-1).astype(np.int64)


def striped8(idx):
    return np.concatenate([x.reshape(-1, 16).T for x in idx]).astype(np.uint16)


def runs(offs, k):
    lists = np.stack([offs[16 * r : 16 * r + 16].T.reshape(-1) for r in range(8)]).astype(np.int64)
    return lists[np.arange(k) % 512 // 64]


def pack_weight(w):
    k, n = w.shape
    w = f64(np.asarray(w, np.float32).astype(ml_dtypes.bfloat16)).reshape(k // 32, 32, n)
    amax = np.abs(w).max(1)
    byte = np.clip(np.where(amax > 0, np.frexp(amax)[1] - 1 + 127 - 7, 1), 1, 254)
    scaled = (w * np.exp2(127.0 - byte)[:, None, :]).reshape(k, n).astype(np.float32)
    words = np.ascontiguousarray(scaled.reshape(k // 512, 128, 4, n).transpose(0, 1, 3, 2)).astype(ml_dtypes.float8_e4m3fn).view(np.uint8)
    return words, np.ascontiguousarray(byte.astype(np.uint8).reshape(k // 512, 16, n))


def unpack_weight(words, scales):
    g, p, n, _ = words.shape
    vals = np.ascontiguousarray(words).view(ml_dtypes.float8_e4m3fn).astype(np.float64) * np.repeat(np.exp2(scales.astype(np.float64) - 127.0), 8, axis=1)[..., None]
    return vals.transpose(0, 1, 3, 2).reshape(g * 512, n)


def sigmoid(v):
    return 1.0 / (1.0 + np.exp(-np.maximum(v, -700.0)))

def planes(y):
    n, m = y.shape
    v = y.astype(np.float32).astype(ml_dtypes.bfloat16).astype(np.float64).reshape(n // 32, 32, m)
    top = np.abs(v).max(1)
    byte = np.clip(np.where(top > 0, np.frexp(top)[1] - 1 + 127 - 7, 1), 1, 254)
    codes = (v * np.exp2(127.0 - byte)[:, None, :]).reshape(n, m).astype(np.float32).astype(ml_dtypes.float8_e4m3fn).view(np.uint8)
    words = codes.reshape(n // 512, 128, 4, m).transpose(0, 1, 3, 2)
    return np.ascontiguousarray(words), np.ascontiguousarray(byte.astype(np.uint8).reshape(n // 512, 16, m))


K, T, S, H, G = 512, 2048, 512, 512, 2048
P = 2 ** 7


def setup_inputs():
    n = np.random.standard_normal
    s = mx_kscale(K)[:, None]
    packed_xT = pack_weight(n((K, T)) * s)
    packed_w1 = pack_weight(n((K, H)) / np.sqrt(K) / s)
    packed_dT = pack_weight(n((K, G)) / s)
    return {
        "x_words": packed_xT[0],
        "x_scales": packed_xT[1],
        "w1_words": packed_w1[0],
        "w1_scales": packed_w1[1],
        "cr": np.tile(np.random.uniform(0.0, 1.0, S), (P, 1)).astype(np.float32),
        "gs": (np.random.uniform(0.5, 1.5, (K, 1)) * s).astype(np.float32),
        "d_words": packed_dT[0],
        "d_scales": packed_dT[1],
        "offs": striped(np.random.permutation(T)[:S]),
        "r1": striped8(np.stack([np.random.permutation(S) for _ in range(8)])),
        "r2": striped8(np.stack([np.random.permutation(S) for _ in range(8)])),
        "r3": striped8(np.stack([np.random.permutation(S) for _ in range(8)])),
        "kq": striped8(np.random.randint(0, G, (8, H))),
    }


def reference(x_words, x_scales, w1_words, w1_scales, cr, gs, d_words, d_scales, offs, r1, r2, r3, kq):
    d_kq = unpack_weight(d_words, d_scales)[np.arange(K)[:, None], runs(kq, K)]
    xq = unpack_weight(x_words, x_scales)[:, unstriped(offs)]
    y = unpack_weight(w1_words, w1_scales).T @ xq
    v1 = y[np.arange(H)[:, None], runs(r1, H)] + 0.5 * (y[np.arange(H)[:, None], runs(r2, H)] - (y[np.arange(H)[:, None], runs(r3, H)]))
    tr = y + f64(cr)[:1] * (v1 - y)
    z = f64(gs) * (tr * sigmoid(tr - y))
    out_0 = 0.0625 * ((d_kq.T @ mxq(z, 0, "e4m3")))
    return (out_0,) + planes(out_0)

@@ -1,0 +1,175 @@
+from contextlib import ExitStack
+
+import concourse.mybir as mybir
+
+K, T, S, H, G = 512, 2048, 512, 512, 2048
+FLOPS = 2 * K * H * S + 2 * H * H * S
+
+F32 = mybir.dt.float32
+BF16 = mybir.dt.bfloat16
+I32 = mybir.dt.int32
+U32 = mybir.dt.uint32
+U16 = mybir.dt.uint16
+U8 = mybir.dt.uint8
+FP8X4 = mybir.dt.float8_e4m3fn_x4
+ALU = mybir.AluOpType
+ACT = mybir.ActivationFunctionType
+
+P = 128
+PACK = 4
+BLOCK = 128
+CHUNKS = (256, 128, 128)
+
+
+def tile_picked_diffevo_none_po_kernel(
+    tc, x_words, x_scales, w1_words, w1_scales, cr, gs, d_words, d_scales, offs, r1, r2, r3, kq, out_0, out_1, out_2
+):
+    nc = tc.nc
+
+    def words_of(dram):
+        return dram[0].rearrange("p n t -> p (n t)").bitcast(I32)
+
+    with ExitStack() as ctx:
+        keep = ctx.enter_context(tc.tile_pool(name="keep", bufs=1))
+        psum = ctx.enter_context(tc.psum_pool(name="psum", bufs=1))
+
+        def sb(name, shape, dtype, tag=None):
+            return keep.tile(shape, dtype, name=name, tag=tag or name, align_bytes=64)
+
+
+        offs_t = sb("offs_t", [P, S // 16], U16)
+        r1_t = sb("r1_t", [P, S // 16], U16)
+        r2_t = sb("r2_t", [P, S // 16], U16)
+        r3_t = sb("r3_t", [P, S // 16], U16)
+        kq_t = sb("kq_t", [P, H // 16], U16)
+
+        xs_win = sb("xs_win", [P, T], U8, tag="xs_cr")
+        ds_win = sb("ds_win", [P, G], U8)
+        w1s_raw = sb("w1s_raw", [P, H], U8)
+        ds_fin = sb("ds_fin", [P, H], U8)
+        xw_win = sb("xw_win", [P, T], U32)
+        w1w_raw = sb("w1w_raw", [P, H], U32, tag="words_in")
+        gs_t = sb("gs_t", [P, PACK], F32)
+
+        warm_in = sb("warm_in", [P, 1], F32)
+        warm_out = sb("warm_out", [P, 1], F32)
+        nc.gpsimd.memset(warm_in[:], 0.0)
+        nc.scalar.activation(warm_out[:], warm_in[:], ACT.Sigmoid)
+        nc.gpsimd.memset(xs_win[:].bitcast(I32), 0)
+        nc.gpsimd.memset(w1s_raw[:].bitcast(I32), 0)
+        nc.vector.memset(ds_win[:].bitcast(I32), 0)
+        nc.vector.memset(ds_fin[:].bitcast(I32), 0)
+
+        nc.sync.dma_start(offs_t[:], offs)
+        nc.sync.dma_start(kq_t[:], kq)
+        nc.sync.dma_start(r3_t[:], r3)
+        nc.sync.dma_start(r2_t[:], r2)
+        nc.sync.dma_start(r1_t[:], r1)
+        nc.sync.dma_start(w1w_raw[:].bitcast(I32), words_of(w1_words))
+        nc.sync.dma_start(xw_win[:].bitcast(I32), words_of(x_words))
+        for q in range(4):
+            nc.sync.dma_start(xs_win[32 * q : 32 * q + 4, :].bitcast(I32), x_scales[0, 4 * q : 4 * q + 4, :].bitcast(I32))
+        for q in range(4):
+            eng = nc.gpsimd if q == 3 else nc.sync
+            eng.dma_start(w1s_raw[32 * q : 32 * q + 4, :].bitcast(I32), w1_scales[0, 4 * q : 4 * q + 4, :].bitcast(I32))
+        nc.sync.dma_start(ds_win[0:P:8, :].bitcast(I32), d_scales[0].bitcast(I32))
+        nc.gpsimd.dma_start(gs_t[:], gs.rearrange("(p t) o -> p (t o)", t=PACK))
+
+        w1w = sb("w1w", [P, PACK, P], U32)
+        w1s = sb("w1s", [P, PACK, P], U8)
+        xs = sb("xs", [P, S], U8)
+        xw = sb("xw", [P, S], U32)
+        nc.vector.tensor_copy(xs[:], xs_win[:].indirect(offs_t[:]))
+        nc.vector.tensor_copy(w1w[:], w1w_raw[:].rearrange("p (m t) -> p t m", t=PACK))
+        nc.vector.tensor_copy(w1s[:], w1s_raw[:].rearrange("p (m t) -> p t m", t=PACK))
+
+        nc.vector.tensor_copy(xw[:], xw_win[:].indirect(offs_t[:]))
+        dw_win = sb("dw_win", [P, G], U32, tag="words_in")
+        cr_t = sb("cr_t", [P, S], F32, tag="xs_cr")
+        nc.sync.dma_start(cr_t[:], cr)
+        nc.sync.dma_start(dw_win[:].bitcast(I32), words_of(d_words))
+        y_full, y_half, y_gs = [], [], []
+        banks = []
+        for t in range(PACK):
+            bank = psum.tile([P, S], F32, name="y_bank%d" % t)
+            nc.tensor.matmul_mx(
+                out=bank[:], lhsT=w1w[:, t, :].bitcast(FP8X4), lhsT_scale=w1s[:, t, :],
+                rhs=xw[:].bitcast(FP8X4), rhs_scale=xs[:], start=True, stop=True,
+            )
+            banks.append(bank)
+            y_full.append(sb("y_full%d" % t, [P, S], F32))
+            y_half.append(sb("y_half%d" % t, [P, S], F32))
+            y_gs.append(sb("y_gs%d" % t, [P, S], F32))
+            nc.scalar.activation(y_half[t][:], bank[:], ACT.Copy, scale=0.5)
+            nc.scalar.copy(y_full[t][:], bank[:])
+        for t in range(PACK):
+            nc.scalar.activation(y_gs[t][:], banks[t][:], ACT.Copy, scale=gs_t[:, t : t + 1])
+
+        ds_g = sb("ds_g", [P, H], U8)
+        dw_g = sb("dw_g", [P, H], U32)
+        ds_d = sb("ds_d", [P, PACK, P], U8)
+        dw = sb("dw", [P, PACK, P], U32)
+        nc.vector.tensor_copy(ds_g[:], ds_win[:].indirect(kq_t[:]))
+        nc.vector.tensor_copy(dw_g[:], dw_win[:].indirect(kq_t[:]))
+        nc.vector.tensor_copy(ds_d[:], ds_g[:].rearrange("p (m t) -> p t m", t=PACK))
+        nc.vector.tensor_copy(dw[:], dw_g[:].rearrange("p (m t) -> p t m", t=PACK))
+        ds_flat = ds_d[:].rearrange("p t m -> p (t m)")
+        for r in range(4):
+            nc.sync.dma_start(ds_fin[r:P:32, :].bitcast(I32), ds_flat[8 * r : P : 32, :].bitcast(I32))
+
+        out_words = sb("out_words", [P, S], U32)
+        out_scales = sb("out_scales", [P, S], U8)
+        out_rows = out_0.rearrange("(p t) j -> p t j", t=PACK)
+
+        c0 = 0
+        for ci, n in enumerate(CHUNKS):
+            cols = slice(c0, c0 + n)
+            lst = slice(c0 // 16, (c0 + n) // 16)
+            a = sb("a%d" % ci, [P, PACK, n], F32)
+            b = sb("b%d" % ci, [P, PACK, n], F32)
+            d = sb("d%d" % ci, [P, PACK, n], F32)
+            u = sb("u%d" % ci, [P, PACK, n], F32)
+            s = sb("s%d" % ci, [P, PACK, n], F32)
+            tr = sb("tr%d" % ci, [P, PACK, n], F32)
+            zb = sb("zb%d" % ci, [P, n, PACK], BF16)
+            zw = sb("zw%d" % ci, [P, n], U32)
+            zs = sb("zs%d" % ci, [P, n], U8)
+            for t in range(PACK):
+                nc.vector.tensor_tensor(a[:, t, :], y_half[t][:].indirect(r3_t[:, lst]), y_full[t][:, cols], ALU.add)
+            for t in range(PACK):
+                nc.vector.tensor_tensor(b[:, t, :], y_half[t][:].indirect(r2_t[:, lst]), a[:, t, :], ALU.subtract)
+            for t in range(PACK):
+                nc.vector.tensor_tensor(d[:, t, :], y_full[t][:].indirect(r1_t[:, lst]), b[:, t, :], ALU.add)
+            nc.vector.tensor_tensor(u[:], d[:], cr_t[:, cols].unsqueeze(1).to_broadcast([P, PACK, n]), ALU.mult)
+            nc.scalar.activation(s[:], u[:], ACT.Sigmoid)
+            for t in range(PACK):
+                nc.vector.scalar_tensor_tensor(tr[:, t, :], u[:, t, :], gs_t[:, t : t + 1], y_gs[t][:, cols], ALU.mult, ALU.add)
+            nc.vector.tensor_tensor(
+                zb[:].rearrange("p (c i) t -> p c t i", i=4),
+                tr[:].rearrange("p t (c i) -> p c t i", i=4),
+                s[:].rearrange("p t (c i) -> p c t i", i=4),
+                ALU.mult,
+            )
+            nc.vector.quantize_mx(out=zw[:].bitcast(FP8X4), scales=zs[:], in_=zb[:].rearrange("p j t -> p (j t)"))
+            for b0 in range(0, n, BLOCK):
+                j0 = c0 + b0
+                blk = slice(j0, j0 + BLOCK)
+                bank = psum.tile([P, PACK, BLOCK], F32, name="o_bank%d" % (j0 // BLOCK))
+                for t in range(PACK):
+                    nc.tensor.matmul_mx(
+                        out=bank[:, t, :], lhsT=dw[:, t, :].bitcast(FP8X4), lhsT_scale=ds_fin[:, t * P : (t + 1) * P],
+                        rhs=zw[:, b0 : b0 + BLOCK].bitcast(FP8X4), rhs_scale=zs[:, b0 : b0 + BLOCK], start=True, stop=True,
+                    )
+                o32 = sb("o32_%d" % j0, [P, PACK, BLOCK], F32)
+                ob = sb("ob_%d" % j0, [P, BLOCK, PACK], BF16)
+                nc.scalar.activation(ob[:], bank[:].rearrange("p t j -> p j t"), ACT.Copy, scale=0.0625)
+                nc.scalar.activation(o32[:], bank[:], ACT.Copy, scale=0.0625)
+                nc.sync.dma_start(out_rows[:, :, blk], o32[:])
+                nc.vector.quantize_mx(
+                    out=out_words[:, blk].bitcast(FP8X4), scales=out_scales[:, blk], in_=ob[:].rearrange("p j t -> p (j t)")
+                )
+                nc.sync.dma_start(words_of(out_1)[:, blk], out_words[:, blk].bitcast(I32))
+            c0 += n
+        for q in range(4):
+            eng = nc.scalar if q % 2 else nc.sync
+            eng.dma_start(out_2[0, 4 * q : 4 * q + 4, :].bitcast(I32), out_scales[32 * q : 32 * q + 4, :].bitcast(I32))

@@ -1,6 +1,7 @@
 from contextlib import ExitStack
 
 import concourse.mybir as mybir
+from concourse.masks import make_identity
 
 K, T, S, H, G = 512, 2048, 512, 512, 2048
 FLOPS = 2 * K * H * S + 2 * H * H * S
@@ -18,7 +19,7 @@ ACT = mybir.ActivationFunctionType
 P = 128
 PACK = 4
 BLOCK = 128
-CHUNKS = (256, 128, 128)
+HALF = 256
 
 
 def tile_picked_diffevo_none_po_kernel(
@@ -36,6 +37,8 @@ def tile_picked_diffevo_none_po_kernel(
         def sb(name, shape, dtype, tag=None):
             return keep.tile(shape, dtype, name=name, tag=tag or name, align_bytes=64)
 
+        def ps(name, shape, bank):
+            return psum.tile(shape, F32, name=name, tag="bank%d" % bank)
 
         offs_t = sb("offs_t", [P, S // 16], U16)
         r1_t = sb("r1_t", [P, S // 16], U16)
@@ -45,74 +48,73 @@ def tile_picked_diffevo_none_po_kernel(
 
         xs_win = sb("xs_win", [P, T], U8, tag="xs_cr")
         ds_win = sb("ds_win", [P, G], U8)
-        w1s_raw = sb("w1s_raw", [P, H], U8)
+        w1s_raw = sb("w1s_raw", [P, H], U8, tag="scales_in")
         ds_fin = sb("ds_fin", [P, H], U8)
-        xw_win = sb("xw_win", [P, T], U32)
+        xw_win = sb("xw_win", [P, T], U32, tag="xw_in")
         w1w_raw = sb("w1w_raw", [P, H], U32, tag="words_in")
-        gs_t = sb("gs_t", [P, PACK], F32)
+        ident = sb("ident", [P, P], F32)
 
         warm_in = sb("warm_in", [P, 1], F32)
         warm_out = sb("warm_out", [P, 1], F32)
-        nc.gpsimd.memset(warm_in[:], 0.0)
-        nc.scalar.activation(warm_out[:], warm_in[:], ACT.Sigmoid)
-        nc.gpsimd.memset(xs_win[:].bitcast(I32), 0)
+        nc.vector.memset(xs_win[:].bitcast(I32), 0)
         nc.gpsimd.memset(w1s_raw[:].bitcast(I32), 0)
-        nc.vector.memset(ds_win[:].bitcast(I32), 0)
-        nc.vector.memset(ds_fin[:].bitcast(I32), 0)
+        nc.gpsimd.memset(ds_win[:].bitcast(I32), 0)
+        nc.gpsimd.memset(warm_in[:], 0.0)
+        nc.gpsimd.memset(ds_fin[:].bitcast(I32), 0)
+        nc.scalar.activation(warm_out[:], warm_in[:], ACT.Sigmoid)
 
         nc.sync.dma_start(offs_t[:], offs)
-        nc.sync.dma_start(kq_t[:], kq)
-        nc.sync.dma_start(r3_t[:], r3)
-        nc.sync.dma_start(r2_t[:], r2)
-        nc.sync.dma_start(r1_t[:], r1)
-        nc.sync.dma_start(w1w_raw[:].bitcast(I32), words_of(w1_words))
-        nc.sync.dma_start(xw_win[:].bitcast(I32), words_of(x_words))
         for q in range(4):
             nc.sync.dma_start(xs_win[32 * q : 32 * q + 4, :].bitcast(I32), x_scales[0, 4 * q : 4 * q + 4, :].bitcast(I32))
+        nc.sync.dma_start(w1w_raw[:].bitcast(I32), words_of(w1_words))
+        nc.sync.dma_start(kq_t[:], kq)
+        nc.sync.dma_start(xw_win[:].bitcast(I32), words_of(x_words))
         for q in range(4):
-            eng = nc.gpsimd if q == 3 else nc.sync
-            eng.dma_start(w1s_raw[32 * q : 32 * q + 4, :].bitcast(I32), w1_scales[0, 4 * q : 4 * q + 4, :].bitcast(I32))
+            nc.sync.dma_start(w1s_raw[32 * q : 32 * q + 4, :].bitcast(I32), w1_scales[0, 4 * q : 4 * q + 4, :].bitcast(I32))
         nc.sync.dma_start(ds_win[0:P:8, :].bitcast(I32), d_scales[0].bitcast(I32))
-        nc.gpsimd.dma_start(gs_t[:], gs.rearrange("(p t) o -> p (t o)", t=PACK))
+        nc.sync.dma_start(r1_t[:], r1)
+        nc.sync.dma_start(r2_t[:], r2)
+        nc.sync.dma_start(r3_t[:], r3)
+        make_identity(nc, ident[:])
 
         w1w = sb("w1w", [P, PACK, P], U32)
         w1s = sb("w1s", [P, PACK, P], U8)
         xs = sb("xs", [P, S], U8)
         xw = sb("xw", [P, S], U32)
-        nc.vector.tensor_copy(xs[:], xs_win[:].indirect(offs_t[:]))
         nc.vector.tensor_copy(w1w[:], w1w_raw[:].rearrange("p (m t) -> p t m", t=PACK))
+        nc.vector.tensor_copy(xs[:], xs_win[:].indirect(offs_t[:]))
+        nc.vector.tensor_copy(xw[:], xw_win[:].indirect(offs_t[:]))
         nc.vector.tensor_copy(w1s[:], w1s_raw[:].rearrange("p (m t) -> p t m", t=PACK))
 
-        nc.vector.tensor_copy(xw[:], xw_win[:].indirect(offs_t[:]))
+        gs_t = sb("gs_t", [P, PACK], F32, tag="scales_in")
+        nc.sync.dma_start(gs_t[:], gs.rearrange("(p t) o -> p (t o)", t=PACK))
         dw_win = sb("dw_win", [P, G], U32, tag="words_in")
-        cr_t = sb("cr_t", [P, S], F32, tag="xs_cr")
-        nc.sync.dma_start(cr_t[:], cr)
+        cr_t = sb("cr_t", [P, S // BLOCK], F32, tag="xs_cr")
+        gs_h = sb("gs_h", [P, PACK], F32)
+        with nc.allow_non_contiguous_dma(reason="one value of cr for each partition and block"):
+            nc.sync.dma_start(cr_t[:], cr[0:1, :].rearrange("o (c p) -> p (o c)", p=P))
         nc.sync.dma_start(dw_win[:].bitcast(I32), words_of(d_words))
-        y_full, y_half, y_gs = [], [], []
-        banks = []
+        nc.gpsimd.tensor_scalar(gs_h[:], gs_t[:], -0.5, 0.0, ALU.mult, ALU.add)
+
+        y_full, y_gs, y_banks = [], [], []
         for t in range(PACK):
-            bank = psum.tile([P, S], F32, name="y_bank%d" % t)
+            bank = ps("y_bank%d" % t, [P, S], t)
             nc.tensor.matmul_mx(
                 out=bank[:], lhsT=w1w[:, t, :].bitcast(FP8X4), lhsT_scale=w1s[:, t, :],
                 rhs=xw[:].bitcast(FP8X4), rhs_scale=xs[:], start=True, stop=True,
             )
-            banks.append(bank)
+            y_banks.append(bank)
             y_full.append(sb("y_full%d" % t, [P, S], F32))
-            y_half.append(sb("y_half%d" % t, [P, S], F32))
             y_gs.append(sb("y_gs%d" % t, [P, S], F32))
-            nc.scalar.activation(y_half[t][:], bank[:], ACT.Copy, scale=0.5)
             nc.scalar.copy(y_full[t][:], bank[:])
         for t in range(PACK):
-            nc.scalar.activation(y_gs[t][:], banks[t][:], ACT.Copy, scale=gs_t[:, t : t + 1])
+            nc.scalar.activation(y_gs[t][:], y_banks[t][:], ACT.Copy, scale=gs_t[:, t : t + 1])
 
-        ds_g = sb("ds_g", [P, H], U8)
-        dw_g = sb("dw_g", [P, H], U32)
+        ds_g = sb("ds_g", [P, H], U8, tag="xw_in")
         ds_d = sb("ds_d", [P, PACK, P], U8)
         dw = sb("dw", [P, PACK, P], U32)
         nc.vector.tensor_copy(ds_g[:], ds_win[:].indirect(kq_t[:]))
-        nc.vector.tensor_copy(dw_g[:], dw_win[:].indirect(kq_t[:]))
         nc.vector.tensor_copy(ds_d[:], ds_g[:].rearrange("p (m t) -> p t m", t=PACK))
-        nc.vector.tensor_copy(dw[:], dw_g[:].rearrange("p (m t) -> p t m", t=PACK))
         ds_flat = ds_d[:].rearrange("p t m -> p (t m)")
         for r in range(4):
             nc.sync.dma_start(ds_fin[r:P:32, :].bitcast(I32), ds_flat[8 * r : P : 32, :].bitcast(I32))
@@ -121,29 +123,54 @@ def tile_picked_diffevo_none_po_kernel(
         out_scales = sb("out_scales", [P, S], U8)
         out_rows = out_0.rearrange("(p t) j -> p t j", t=PACK)
 
-        c0 = 0
-        for ci, n in enumerate(CHUNKS):
-            cols = slice(c0, c0 + n)
-            lst = slice(c0 // 16, (c0 + n) // 16)
-            a = sb("a%d" % ci, [P, PACK, n], F32)
-            b = sb("b%d" % ci, [P, PACK, n], F32)
-            d = sb("d%d" % ci, [P, PACK, n], F32)
-            u = sb("u%d" % ci, [P, PACK, n], F32)
-            s = sb("s%d" % ci, [P, PACK, n], F32)
-            tr = sb("tr%d" % ci, [P, PACK, n], F32)
-            zb = sb("zb%d" % ci, [P, n, PACK], BF16)
-            zw = sb("zw%d" % ci, [P, n], U32)
-            zs = sb("zs%d" % ci, [P, n], U8)
+        def first(c0):
+            lst = slice(c0 // 16, (c0 + HALF) // 16)
+            a = sb("a%d" % c0, [P, PACK, HALF], F32)
             for t in range(PACK):
-                nc.vector.tensor_tensor(a[:, t, :], y_half[t][:].indirect(r3_t[:, lst]), y_full[t][:, cols], ALU.add)
+                nc.vector.tensor_scalar(a[:, t, :], y_full[t][:].indirect(r1_t[:, lst]), 2.0, 0.0, ALU.mult, ALU.add)
+            return a
+
+        def rest(c0, a):
+            lst = slice(c0 // 16, (c0 + HALF) // 16)
+            b = sb("b%d" % c0, [P, PACK, HALF], F32, tag="b")
+            e = sb("e%d" % c0, [P, PACK, HALF], F32)
             for t in range(PACK):
-                nc.vector.tensor_tensor(b[:, t, :], y_half[t][:].indirect(r2_t[:, lst]), a[:, t, :], ALU.subtract)
+                nc.vector.tensor_tensor(b[:, t, :], y_full[t][:].indirect(r2_t[:, lst]), a[:, t, :], ALU.add)
             for t in range(PACK):
-                nc.vector.tensor_tensor(d[:, t, :], y_full[t][:].indirect(r1_t[:, lst]), b[:, t, :], ALU.add)
-            nc.vector.tensor_tensor(u[:], d[:], cr_t[:, cols].unsqueeze(1).to_broadcast([P, PACK, n]), ALU.mult)
-            nc.scalar.activation(s[:], u[:], ACT.Sigmoid)
+                nc.vector.tensor_tensor(e[:, t, :], y_full[t][:].indirect(r3_t[:, lst]), b[:, t, :], ALU.subtract)
+            return e
+
+        def turn(j0, e):
+            blk = j0 // BLOCK
+            b0 = j0 % HALF
+            d_bank = ps("d_bank%d" % blk, [P, PACK, P], 4 + blk % 2)
             for t in range(PACK):
-                nc.vector.scalar_tensor_tensor(tr[:, t, :], u[:, t, :], gs_t[:, t : t + 1], y_gs[t][:, cols], ALU.mult, ALU.add)
+                y_blk = y_full[t][:, j0 : j0 + BLOCK]
+                nc.tensor.matmul(d_bank[:, t, :], y_blk, ident[:], start=True, stop=False, is_transpose=True)
+                nc.tensor.matmul(d_bank[:, t, :], y_blk, ident[:], start=False, stop=False, is_transpose=True)
+                nc.tensor.matmul(d_bank[:, t, :], e[:, t, b0 : b0 + BLOCK], ident[:], start=False, stop=True, is_transpose=True)
+            ut = sb("ut%d" % blk, [P, PACK, P], F32)
+            nc.scalar.activation(ut[:], d_bank[:], ACT.Copy, scale=cr_t[:, blk : blk + 1])
+            return ut
+
+        def cross(c0, u_turned, u_banks):
+            n = BLOCK * len(u_turned)
+            per_bank = 512 // n
+            s = sb("s%d" % c0, [P, PACK, n], F32)
+            tr = sb("tr%d" % c0, [P, PACK, n], F32)
+            for t0, bank_no in zip(range(0, PACK, per_bank), u_banks):
+                u_bank = ps("u_bank%d_%d" % (c0, t0), [P, per_bank, n], bank_no)
+                for t in range(t0, t0 + per_bank):
+                    for i, ut in enumerate(u_turned):
+                        nc.tensor.transpose(u_bank[:, t - t0, i * BLOCK : (i + 1) * BLOCK], ut[:, t, :], ident[:])
+                nc.scalar.activation(s[:, t0 : t0 + per_bank, :], u_bank[:], ACT.Sigmoid, scale=-0.5)
+                for t in range(t0, t0 + per_bank):
+                    nc.vector.scalar_tensor_tensor(
+                        tr[:, t, :], u_bank[:, t - t0, :], gs_h[:, t : t + 1], y_gs[t][:, c0 : c0 + n], ALU.mult, ALU.add
+                    )
+            zb = sb("zb%d" % c0, [P, n, PACK], BF16)
+            zw = sb("zw%d" % c0, [P, n], U32)
+            zs = sb("zs%d" % c0, [P, n], U8)
             nc.vector.tensor_tensor(
                 zb[:].rearrange("p (c i) t -> p c t i", i=4),
                 tr[:].rearrange("p t (c i) -> p c t i", i=4),
@@ -151,25 +178,62 @@ def tile_picked_diffevo_none_po_kernel(
                 ALU.mult,
             )
             nc.vector.quantize_mx(out=zw[:].bitcast(FP8X4), scales=zs[:], in_=zb[:].rearrange("p j t -> p (j t)"))
-            for b0 in range(0, n, BLOCK):
-                j0 = c0 + b0
-                blk = slice(j0, j0 + BLOCK)
-                bank = psum.tile([P, PACK, BLOCK], F32, name="o_bank%d" % (j0 // BLOCK))
-                for t in range(PACK):
-                    nc.tensor.matmul_mx(
-                        out=bank[:, t, :], lhsT=dw[:, t, :].bitcast(FP8X4), lhsT_scale=ds_fin[:, t * P : (t + 1) * P],
-                        rhs=zw[:, b0 : b0 + BLOCK].bitcast(FP8X4), rhs_scale=zs[:, b0 : b0 + BLOCK], start=True, stop=True,
-                    )
-                o32 = sb("o32_%d" % j0, [P, PACK, BLOCK], F32)
-                ob = sb("ob_%d" % j0, [P, BLOCK, PACK], BF16)
-                nc.scalar.activation(ob[:], bank[:].rearrange("p t j -> p j t"), ACT.Copy, scale=0.0625)
-                nc.scalar.activation(o32[:], bank[:], ACT.Copy, scale=0.0625)
-                nc.sync.dma_start(out_rows[:, :, blk], o32[:])
-                nc.vector.quantize_mx(
-                    out=out_words[:, blk].bitcast(FP8X4), scales=out_scales[:, blk], in_=ob[:].rearrange("p j t -> p (j t)")
-                )
-                nc.sync.dma_start(words_of(out_1)[:, blk], out_words[:, blk].bitcast(I32))
-            c0 += n
+            return zw, zs
+
+        def product(acc, t, zw, zs):
+            nc.tensor.matmul_mx(
+                out=acc, lhsT=dw[:, t, :].bitcast(FP8X4), lhsT_scale=ds_fin[:, t * P : (t + 1) * P],
+                rhs=zw.bitcast(FP8X4), rhs_scale=zs, start=True, stop=True,
+            )
+
+        def store(j0, o32, ob):
+            blk = slice(j0, j0 + BLOCK)
+            nc.sync.dma_start(out_rows[:, :, blk], o32[:])
+            nc.vector.quantize_mx(
+                out=out_words[:, blk].bitcast(FP8X4), scales=out_scales[:, blk], in_=ob[:].rearrange("p j t -> p (j t)")
+            )
+            nc.sync.dma_start(words_of(out_1)[:, blk], out_words[:, blk].bitcast(I32))
+
+        def finish(j0, zw, zs, bank_no):
+            bank = ps("o_bank%d" % j0, [P, PACK, BLOCK], bank_no)
+            for t in range(PACK):
+                product(bank[:, t, :], t, zw, zs)
+            o32 = sb("o32_%d" % j0, [P, PACK, BLOCK], F32)
+            ob = sb("ob_%d" % j0, [P, BLOCK, PACK], BF16)
+            nc.scalar.activation(o32[:], bank[:], ACT.Copy, scale=0.0625)
+            nc.scalar.activation(ob[:], bank[:].rearrange("p t j -> p j t"), ACT.Copy, scale=0.0625)
+            store(j0, o32, ob)
+
+        def finish_last(j0, zw, zs, bank_nos):
+            o32 = sb("o32_%d" % j0, [P, PACK, BLOCK], F32)
+            ob = sb("ob_%d" % j0, [P, BLOCK, PACK], BF16)
+            lo = ps("o_lo", [P, 2, BLOCK], bank_nos[0])
+            hi = ps("o_hi", [P, 2, BLOCK], bank_nos[1])
+            for t in range(2):
+                product(lo[:, t, :], t, zw, zs)
+            for t in range(2):
+                product(hi[:, t, :], 2 + t, zw, zs)
+            nc.vector.tensor_scalar(o32[:, 0:2, :], lo[:], 0.0625, None, ALU.mult)
+            nc.scalar.activation(o32[:, 2:4, :], hi[:], ACT.Copy, scale=0.0625)
+            nc.vector.tensor_copy(ob[:].rearrange("p (c i) t -> p c t i", i=4), o32[:].rearrange("p t (c i) -> p c t i", i=4))
+            store(j0, o32, ob)
+
+        a0 = first(0)
+        e0 = rest(0, a0)
+        a1 = first(HALF)
+        dw_g = sb("dw_g", [P, H], U32, tag="a0")
+        nc.vector.tensor_copy(dw_g[:], dw_win[:].indirect(kq_t[:]))
+        nc.vector.tensor_copy(dw[:], dw_g[:].rearrange("p (m t) -> p t m", t=PACK))
+        e1 = rest(HALF, a1)
+        ut = [turn(0, e0), turn(BLOCK, e0)]
+        zw0, zs0 = cross(0, ut, (6, 7))
+        ut = [turn(2 * BLOCK, e1), turn(3 * BLOCK, e1)]
+        zw2, zs2 = cross(2 * BLOCK, ut[:1], (2,))
+        finish(0, zw0[:, :BLOCK], zs0[:, :BLOCK], 0)
+        finish(BLOCK, zw0[:, BLOCK:], zs0[:, BLOCK:], 1)
+        zw3, zs3 = cross(3 * BLOCK, ut[1:], (3,))
+        finish(2 * BLOCK, zw2[:], zs2[:], 4)
+        finish_last(3 * BLOCK, zw3[:], zs3[:], (5, 6))
         for q in range(4):
             eng = nc.scalar if q % 2 else nc.sync
             eng.dma_start(out_2[0, 4 * q : 4 * q + 4, :].bitcast(I32), out_scales[32 * q : 32 * q + 4, :].bitcast(I32))

@@ -40,6 +40,11 @@ def tile_picked_diffevo_none_po_kernel(
         def ps(name, shape, bank):
             return psum.tile(shape, F32, name=name, tag="bank%d" % bank)
 
+        def deal_words(dealt, plain):
+            nc.vector.tensor_copy(
+                dealt[:].rearrange("p t (c i) -> p c t i", i=4), plain[:].rearrange("p (c i t) -> p c t i", i=4, t=PACK)
+            )
+
         offs_t = sb("offs_t", [P, S // 16], U16)
         r1_t = sb("r1_t", [P, S // 16], U16)
         r2_t = sb("r2_t", [P, S // 16], U16)
@@ -76,12 +81,13 @@ def tile_picked_diffevo_none_po_kernel(
         nc.sync.dma_start(r2_t[:], r2)
         nc.sync.dma_start(r3_t[:], r3)
         make_identity(nc, ident[:])
+        y_win = [sb("y_win%d" % t, [P, 2 * S], F32) for t in range(PACK)]
 
         w1w = sb("w1w", [P, PACK, P], U32)
         w1s = sb("w1s", [P, PACK, P], U8)
         xs = sb("xs", [P, S], U8)
         xw = sb("xw", [P, S], U32)
-        nc.vector.tensor_copy(w1w[:], w1w_raw[:].rearrange("p (m t) -> p t m", t=PACK))
+        deal_words(w1w, w1w_raw)
         nc.vector.tensor_copy(xs[:], xs_win[:].indirect(offs_t[:]))
         nc.vector.tensor_copy(xw[:], xw_win[:].indirect(offs_t[:]))
         nc.vector.tensor_copy(w1s[:], w1s_raw[:].rearrange("p (m t) -> p t m", t=PACK))
@@ -104,9 +110,9 @@ def tile_picked_diffevo_none_po_kernel(
                 rhs=xw[:].bitcast(FP8X4), rhs_scale=xs[:], start=True, stop=True,
             )
             y_banks.append(bank)
-            y_full.append(sb("y_full%d" % t, [P, S], F32))
+            y_full.append(y_win[t][:, :S])
             y_gs.append(sb("y_gs%d" % t, [P, S], F32))
-            nc.scalar.copy(y_full[t][:], bank[:])
+            nc.scalar.copy(y_full[t], bank[:])
         for t in range(PACK):
             nc.scalar.activation(y_gs[t][:], y_banks[t][:], ACT.Copy, scale=gs_t[:, t : t + 1])
 
@@ -123,62 +129,44 @@ def tile_picked_diffevo_none_po_kernel(
         out_scales = sb("out_scales", [P, S], U8)
         out_rows = out_0.rearrange("(p t) j -> p t j", t=PACK)
 
-        def first(c0):
-            lst = slice(c0 // 16, (c0 + HALF) // 16)
-            a = sb("a%d" % c0, [P, PACK, HALF], F32)
-            for t in range(PACK):
-                nc.vector.tensor_scalar(a[:, t, :], y_full[t][:].indirect(r1_t[:, lst]), 2.0, 0.0, ALU.mult, ALU.add)
-            return a
+        a = [sb("a%d" % t, [P, S], F32) for t in range(PACK)]
+        b = [sb("b%d" % t, [P, S], F32) for t in range(PACK)]
+        e = [sb("e%d" % t, [P, S], F32) for t in range(PACK)]
+        s = sb("s", [P, PACK, S], F32)
+        tr = sb("tr", [P, PACK, S], F32)
 
-        def rest(c0, a):
-            lst = slice(c0 // 16, (c0 + HALF) // 16)
-            b = sb("b%d" % c0, [P, PACK, HALF], F32, tag="b")
-            e = sb("e%d" % c0, [P, PACK, HALF], F32)
-            for t in range(PACK):
-                nc.vector.tensor_tensor(b[:, t, :], y_full[t][:].indirect(r2_t[:, lst]), a[:, t, :], ALU.add)
-            for t in range(PACK):
-                nc.vector.tensor_tensor(e[:, t, :], y_full[t][:].indirect(r3_t[:, lst]), b[:, t, :], ALU.subtract)
-            return e
+        def gather(step, t):
+            if step == 0:
+                nc.vector.tensor_scalar(a[t][:], y_win[t][:].indirect(r1_t[:]), 2.0, 0.0, ALU.mult, ALU.add)
+            elif step == 1:
+                nc.vector.tensor_tensor(b[t][:], y_win[t][:].indirect(r2_t[:]), a[t][:], ALU.add)
+            else:
+                nc.vector.tensor_tensor(e[t][:], y_win[t][:].indirect(r3_t[:]), b[t][:], ALU.subtract)
 
-        def turn(j0, e):
-            blk = j0 // BLOCK
-            b0 = j0 % HALF
-            d_bank = ps("d_bank%d" % blk, [P, PACK, P], 4 + blk % 2)
-            for t in range(PACK):
-                y_blk = y_full[t][:, j0 : j0 + BLOCK]
-                nc.tensor.matmul(d_bank[:, t, :], y_blk, ident[:], start=True, stop=False, is_transpose=True)
-                nc.tensor.matmul(d_bank[:, t, :], y_blk, ident[:], start=False, stop=False, is_transpose=True)
-                nc.tensor.matmul(d_bank[:, t, :], e[:, t, b0 : b0 + BLOCK], ident[:], start=False, stop=True, is_transpose=True)
-            ut = sb("ut%d" % blk, [P, PACK, P], F32)
-            nc.scalar.activation(ut[:], d_bank[:], ACT.Copy, scale=cr_t[:, blk : blk + 1])
-            return ut
+        for wave in range(PACK + 2):
+            for step in range(3):
+                if 0 <= wave - step < PACK:
+                    gather(step, wave - step)
 
-        def cross(c0, u_turned, u_banks):
-            n = BLOCK * len(u_turned)
-            per_bank = 512 // n
-            s = sb("s%d" % c0, [P, PACK, n], F32)
-            tr = sb("tr%d" % c0, [P, PACK, n], F32)
-            for t0, bank_no in zip(range(0, PACK, per_bank), u_banks):
-                u_bank = ps("u_bank%d_%d" % (c0, t0), [P, per_bank, n], bank_no)
-                for t in range(t0, t0 + per_bank):
-                    for i, ut in enumerate(u_turned):
-                        nc.tensor.transpose(u_bank[:, t - t0, i * BLOCK : (i + 1) * BLOCK], ut[:, t, :], ident[:])
-                nc.scalar.activation(s[:, t0 : t0 + per_bank, :], u_bank[:], ACT.Sigmoid, scale=-0.5)
-                for t in range(t0, t0 + per_bank):
-                    nc.vector.scalar_tensor_tensor(
-                        tr[:, t, :], u_bank[:, t - t0, :], gs_h[:, t : t + 1], y_gs[t][:, c0 : c0 + n], ALU.mult, ALU.add
-                    )
-            zb = sb("zb%d" % c0, [P, n, PACK], BF16)
-            zw = sb("zw%d" % c0, [P, n], U32)
-            zs = sb("zs%d" % c0, [P, n], U8)
-            nc.vector.tensor_tensor(
-                zb[:].rearrange("p (c i) t -> p c t i", i=4),
-                tr[:].rearrange("p t (c i) -> p c t i", i=4),
-                s[:].rearrange("p t (c i) -> p c t i", i=4),
-                ALU.mult,
-            )
-            nc.vector.quantize_mx(out=zw[:].bitcast(FP8X4), scales=zs[:], in_=zb[:].rearrange("p j t -> p (j t)"))
-            return zw, zs
+        dw_g = sb("dw_g", [P, H], U32, tag="b3")
+        nc.vector.tensor_copy(dw_g[:], dw_win[:].indirect(kq_t[:]))
+        deal_words(dw, dw_g)
+
+        for t in range(PACK):
+            ut = sb("ut%d" % t, [P, S // BLOCK, P], F32)
+            d_banks = [ps("d_bank%d_%d" % (t, blk), [P, P], 4 + blk) for blk in range(S // BLOCK)]
+            for blk, d_bank in enumerate(d_banks):
+                y_blk = y_full[t][:, blk * BLOCK : (blk + 1) * BLOCK]
+                nc.tensor.matmul(d_bank[:], y_blk, ident[:], start=True, stop=False, is_transpose=True)
+                nc.tensor.matmul(d_bank[:], y_blk, ident[:], start=False, stop=False, is_transpose=True)
+            for blk, d_bank in enumerate(d_banks):
+                nc.tensor.matmul(d_bank[:], e[t][:, blk * BLOCK : (blk + 1) * BLOCK], ident[:], start=False, stop=True, is_transpose=True)
+                nc.scalar.activation(ut[:, blk, :], d_bank[:], ACT.Copy, scale=cr_t[:, blk : blk + 1])
+            u_bank = ps("u_bank%d" % t, [P, S], t)
+            for blk in range(S // BLOCK):
+                nc.tensor.transpose(u_bank[:, blk * BLOCK : (blk + 1) * BLOCK], ut[:, blk, :], ident[:])
+            nc.scalar.activation(s[:, t, :], u_bank[:], ACT.Sigmoid, scale=-0.5)
+            nc.vector.scalar_tensor_tensor(tr[:, t, :], u_bank[:], gs_h[:, t : t + 1], y_gs[t][:], ALU.mult, ALU.add)
 
         def product(acc, t, zw, zs):
             nc.tensor.matmul_mx(
@@ -186,54 +174,51 @@ def tile_picked_diffevo_none_po_kernel(
                 rhs=zw.bitcast(FP8X4), rhs_scale=zs, start=True, stop=True,
             )
 
-        def store(j0, o32, ob):
-            blk = slice(j0, j0 + BLOCK)
-            nc.sync.dma_start(out_rows[:, :, blk], o32[:])
-            nc.vector.quantize_mx(
-                out=out_words[:, blk].bitcast(FP8X4), scales=out_scales[:, blk], in_=ob[:].rearrange("p j t -> p (j t)")
+        n_blocks = S // BLOCK
+        zb = [sb("zb%d" % blk, [P, BLOCK, PACK], BF16) for blk in range(n_blocks)]
+        zw = [sb("zw%d" % blk, [P, BLOCK], U32) for blk in range(n_blocks)]
+        zs = [sb("zs%d" % blk, [P, BLOCK], U8) for blk in range(n_blocks)]
+        o32 = [sb("o32_%d" % blk, [P, PACK, BLOCK], F32) for blk in range(n_blocks)]
+        ob = [sb("ob_%d" % blk, [P, BLOCK, PACK], BF16) for blk in range(n_blocks)]
+
+        def gate(blk):
+            cols = slice(blk * BLOCK, (blk + 1) * BLOCK)
+            nc.vector.tensor_tensor(
+                zb[blk][:].rearrange("p (c i) t -> p c t i", i=4),
+                tr[:, :, cols].rearrange("p t (c i) -> p c t i", i=4),
+                s[:, :, cols].rearrange("p t (c i) -> p c t i", i=4),
+                ALU.mult,
             )
-            nc.sync.dma_start(words_of(out_1)[:, blk], out_words[:, blk].bitcast(I32))
 
-        def finish(j0, zw, zs, bank_no):
-            bank = ps("o_bank%d" % j0, [P, PACK, BLOCK], bank_no)
+        def multiply(blk):
+            cols = slice(blk * BLOCK, (blk + 1) * BLOCK)
+            nc.vector.quantize_mx(out=zw[blk][:].bitcast(FP8X4), scales=zs[blk][:], in_=zb[blk][:].rearrange("p j t -> p (j t)"))
+            bank = ps("o_bank%d" % blk, [P, PACK, BLOCK], 4 + blk)
             for t in range(PACK):
-                product(bank[:, t, :], t, zw, zs)
-            o32 = sb("o32_%d" % j0, [P, PACK, BLOCK], F32)
-            ob = sb("ob_%d" % j0, [P, BLOCK, PACK], BF16)
-            nc.scalar.activation(o32[:], bank[:], ACT.Copy, scale=0.0625)
-            nc.scalar.activation(ob[:], bank[:].rearrange("p t j -> p j t"), ACT.Copy, scale=0.0625)
-            store(j0, o32, ob)
+                product(bank[:, t, :], t, zw[blk][:], zs[blk][:])
+            nc.scalar.activation(o32[blk][:], bank[:], ACT.Copy, scale=0.0625)
+            nc.sync.dma_start(out_rows[:, :, cols], o32[blk][:])
+            if blk == 0:
+                nc.scalar.activation(ob[blk][:], bank[:].rearrange("p t j -> p j t"), ACT.Copy, scale=0.0625)
 
-        def finish_last(j0, zw, zs, bank_nos):
-            o32 = sb("o32_%d" % j0, [P, PACK, BLOCK], F32)
-            ob = sb("ob_%d" % j0, [P, BLOCK, PACK], BF16)
-            lo = ps("o_lo", [P, 2, BLOCK], bank_nos[0])
-            hi = ps("o_hi", [P, 2, BLOCK], bank_nos[1])
-            for t in range(2):
-                product(lo[:, t, :], t, zw, zs)
-            for t in range(2):
-                product(hi[:, t, :], 2 + t, zw, zs)
-            nc.vector.tensor_scalar(o32[:, 0:2, :], lo[:], 0.0625, None, ALU.mult)
-            nc.scalar.activation(o32[:, 2:4, :], hi[:], ACT.Copy, scale=0.0625)
-            nc.vector.tensor_copy(ob[:].rearrange("p (c i) t -> p c t i", i=4), o32[:].rearrange("p t (c i) -> p c t i", i=4))
-            store(j0, o32, ob)
+        def planes(blk):
+            cols = slice(blk * BLOCK, (blk + 1) * BLOCK)
+            if blk > 0:
+                nc.vector.tensor_copy(
+                    ob[blk][:].rearrange("p (c i) t -> p c t i", i=4), o32[blk][:].rearrange("p t (c i) -> p c t i", i=4)
+                )
+            nc.vector.quantize_mx(
+                out=out_words[:, cols].bitcast(FP8X4), scales=out_scales[:, cols], in_=ob[blk][:].rearrange("p j t -> p (j t)")
+            )
+            nc.sync.dma_start(words_of(out_1)[:, cols], out_words[:, cols].bitcast(I32))
 
-        a0 = first(0)
-        e0 = rest(0, a0)
-        a1 = first(HALF)
-        dw_g = sb("dw_g", [P, H], U32, tag="a0")
-        nc.vector.tensor_copy(dw_g[:], dw_win[:].indirect(kq_t[:]))
-        nc.vector.tensor_copy(dw[:], dw_g[:].rearrange("p (m t) -> p t m", t=PACK))
-        e1 = rest(HALF, a1)
-        ut = [turn(0, e0), turn(BLOCK, e0)]
-        zw0, zs0 = cross(0, ut, (6, 7))
-        ut = [turn(2 * BLOCK, e1), turn(3 * BLOCK, e1)]
-        zw2, zs2 = cross(2 * BLOCK, ut[:1], (2,))
-        finish(0, zw0[:, :BLOCK], zs0[:, :BLOCK], 0)
-        finish(BLOCK, zw0[:, BLOCK:], zs0[:, BLOCK:], 1)
-        zw3, zs3 = cross(3 * BLOCK, ut[1:], (3,))
-        finish(2 * BLOCK, zw2[:], zs2[:], 4)
-        finish_last(3 * BLOCK, zw3[:], zs3[:], (5, 6))
+        gate(0)
+        for blk in range(1, n_blocks):
+            gate(blk)
+            multiply(blk - 1)
+        multiply(n_blocks - 1)
+        for blk in range(n_blocks):
+            planes(blk)
         for q in range(4):
             eng = nc.scalar if q % 2 else nc.sync
             eng.dma_start(out_2[0, 4 * q : 4 * q + 4, :].bitcast(I32), out_scales[32 * q : 32 * q + 4, :].bitcast(I32))

@@ -100,7 +100,6 @@ def tile_picked_diffevo_none_po_kernel(
         with nc.allow_non_contiguous_dma(reason="one value of cr for each partition and block"):
             nc.sync.dma_start(cr_t[:], cr[0:1, :].rearrange("o (c p) -> p (o c)", p=P))
         nc.sync.dma_start(dw_win[:].bitcast(I32), words_of(d_words))
-        nc.gpsimd.tensor_scalar(gs_h[:], gs_t[:], -0.5, 0.0, ALU.mult, ALU.add)
 
         y_full, y_gs, y_banks = [], [], []
         for t in range(PACK):
@@ -113,6 +112,7 @@ def tile_picked_diffevo_none_po_kernel(
             y_full.append(y_win[t][:, :S])
             y_gs.append(sb("y_gs%d" % t, [P, S], F32))
             nc.scalar.copy(y_full[t], bank[:])
+        nc.scalar.activation(gs_h[:], gs_t[:], ACT.Copy, scale=-0.5)
         for t in range(PACK):
             nc.scalar.activation(y_gs[t][:], y_banks[t][:], ACT.Copy, scale=gs_t[:, t : t + 1])
 
@@ -162,11 +162,14 @@ def tile_picked_diffevo_none_po_kernel(
             for blk, d_bank in enumerate(d_banks):
                 nc.tensor.matmul(d_bank[:], e[t][:, blk * BLOCK : (blk + 1) * BLOCK], ident[:], start=False, stop=True, is_transpose=True)
                 nc.scalar.activation(ut[:, blk, :], d_bank[:], ACT.Copy, scale=cr_t[:, blk : blk + 1])
-            u_bank = ps("u_bank%d" % t, [P, S], t)
-            for blk in range(S // BLOCK):
-                nc.tensor.transpose(u_bank[:, blk * BLOCK : (blk + 1) * BLOCK], ut[:, blk, :], ident[:])
-            nc.scalar.activation(s[:, t, :], u_bank[:], ACT.Sigmoid, scale=-0.5)
-            nc.vector.scalar_tensor_tensor(tr[:, t, :], u_bank[:], gs_h[:, t : t + 1], y_gs[t][:], ALU.mult, ALU.add)
+            u_banks = [ps("u_bank%d" % t, [P, S], t)]
+            if t == PACK - 1:
+                u_banks.append(ps("u_twin", [P, S], 0))
+            for u_bank in u_banks:
+                for blk in range(S // BLOCK):
+                    nc.tensor.transpose(u_bank[:, blk * BLOCK : (blk + 1) * BLOCK], ut[:, blk, :], ident[:])
+            nc.scalar.activation(s[:, t, :], u_banks[0][:], ACT.Sigmoid, scale=-0.5)
+            nc.vector.scalar_tensor_tensor(tr[:, t, :], u_banks[-1][:], gs_h[:, t : t + 1], y_gs[t][:], ALU.mult, ALU.add)
 
         def product(acc, t, zw, zs):
             nc.tensor.matmul_mx(
@@ -179,14 +182,14 @@ def tile_picked_diffevo_none_po_kernel(
         zw = [sb("zw%d" % blk, [P, BLOCK], U32) for blk in range(n_blocks)]
         zs = [sb("zs%d" % blk, [P, BLOCK], U8) for blk in range(n_blocks)]
         o32 = [sb("o32_%d" % blk, [P, PACK, BLOCK], F32) for blk in range(n_blocks)]
-        ob = [sb("ob_%d" % blk, [P, BLOCK, PACK], BF16) for blk in range(n_blocks)]
+        ob = sb("ob", [P, S, PACK], BF16)
 
         def gate(blk):
             cols = slice(blk * BLOCK, (blk + 1) * BLOCK)
             nc.vector.tensor_tensor(
-                zb[blk][:].rearrange("p (c i) t -> p c t i", i=4),
-                tr[:, :, cols].rearrange("p t (c i) -> p c t i", i=4),
-                s[:, :, cols].rearrange("p t (c i) -> p c t i", i=4),
+                zb[blk][:].rearrange("p (c i) t -> p c t i", i=2),
+                tr[:, :, cols].rearrange("p t (c i) -> p c t i", i=2),
+                s[:, :, cols].rearrange("p t (c i) -> p c t i", i=2),
                 ALU.mult,
             )
 
@@ -198,17 +201,16 @@ def tile_picked_diffevo_none_po_kernel(
                 product(bank[:, t, :], t, zw[blk][:], zs[blk][:])
             nc.scalar.activation(o32[blk][:], bank[:], ACT.Copy, scale=0.0625)
             nc.sync.dma_start(out_rows[:, :, cols], o32[blk][:])
-            if blk == 0:
-                nc.scalar.activation(ob[blk][:], bank[:].rearrange("p t j -> p j t"), ACT.Copy, scale=0.0625)
 
-        def planes(blk):
-            cols = slice(blk * BLOCK, (blk + 1) * BLOCK)
-            if blk > 0:
-                nc.vector.tensor_copy(
-                    ob[blk][:].rearrange("p (c i) t -> p c t i", i=4), o32[blk][:].rearrange("p t (c i) -> p c t i", i=4)
-                )
+        def round_out(blk):
+            nc.vector.tensor_copy(
+                ob[:, blk * BLOCK : (blk + 1) * BLOCK, :].rearrange("p (c i) t -> p c t i", i=2),
+                o32[blk][:].rearrange("p t (c i) -> p c t i", i=2),
+            )
+
+        def planes(cols):
             nc.vector.quantize_mx(
-                out=out_words[:, cols].bitcast(FP8X4), scales=out_scales[:, cols], in_=ob[blk][:].rearrange("p j t -> p (j t)")
+                out=out_words[:, cols].bitcast(FP8X4), scales=out_scales[:, cols], in_=ob[:, cols, :].rearrange("p j t -> p (j t)")
             )
             nc.sync.dma_start(words_of(out_1)[:, cols], out_words[:, cols].bitcast(I32))
 
@@ -218,7 +220,9 @@ def tile_picked_diffevo_none_po_kernel(
             multiply(blk - 1)
         multiply(n_blocks - 1)
         for blk in range(n_blocks):
-            planes(blk)
+            round_out(blk)
+            if blk % 2:
+                planes(slice((blk - 1) * BLOCK, (blk + 1) * BLOCK))
         for q in range(4):
             eng = nc.scalar if q % 2 else nc.sync
             eng.dma_start(out_2[0, 4 * q : 4 * q + 4, :].bitcast(I32), out_scales[32 * q : 32 * q + 4, :].bitcast(I32))

@@ -18,8 +18,11 @@ ACT = mybir.ActivationFunctionType
 
 P = 128
 PACK = 4
+QUADRANTS = 4
 BLOCK = 128
-HALF = 256
+N_BLOCKS = S // BLOCK
+LAST = PACK - 1
+OUT_SCALE = 0.0625
 
 
 def tile_picked_diffevo_none_po_kernel(
@@ -29,6 +32,9 @@ def tile_picked_diffevo_none_po_kernel(
 
     def words_of(dram):
         return dram[0].rearrange("p n t -> p (n t)").bitcast(I32)
+
+    def block(blk):
+        return slice(blk * BLOCK, (blk + 1) * BLOCK)
 
     with ExitStack() as ctx:
         keep = ctx.enter_context(tc.tile_pool(name="keep", bufs=1))
@@ -45,43 +51,44 @@ def tile_picked_diffevo_none_po_kernel(
                 dealt[:].rearrange("p t (c i) -> p c t i", i=4), plain[:].rearrange("p (c i t) -> p c t i", i=4, t=PACK)
             )
 
+        def deal_bytes(dealt, plain):
+            nc.vector.tensor_copy(dealt[:], plain[:].rearrange("p (m t) -> p t m", t=PACK))
+
         offs_t = sb("offs_t", [P, S // 16], U16)
         r1_t = sb("r1_t", [P, S // 16], U16)
         r2_t = sb("r2_t", [P, S // 16], U16)
         r3_t = sb("r3_t", [P, S // 16], U16)
         kq_t = sb("kq_t", [P, H // 16], U16)
 
-        xs_win = sb("xs_win", [P, T], U8, tag="xs_cr")
+        xs_win = sb("xs_win", [P, T], U8, tag="x_scales_then_cr")
         ds_win = sb("ds_win", [P, G], U8)
-        w1s_raw = sb("w1s_raw", [P, H], U8, tag="scales_in")
-        ds_fin = sb("ds_fin", [P, H], U8)
-        xw_win = sb("xw_win", [P, T], U32, tag="xw_in")
-        w1w_raw = sb("w1w_raw", [P, H], U32, tag="words_in")
+        w1s_raw = sb("w1s_raw", [P, H], U8, tag="w1_scales_then_gs")
+        ds = sb("ds", [P, H], U8)
+        xw_win = sb("xw_win", [P, T], U32, tag="x_words_then_d_scales")
+        w1w_raw = sb("w1w_raw", [P, H], U32, tag="w1_words_then_d_words")
         ident = sb("ident", [P, P], F32)
 
-        warm_in = sb("warm_in", [P, 1], F32)
-        warm_out = sb("warm_out", [P, 1], F32)
         nc.vector.memset(xs_win[:].bitcast(I32), 0)
         nc.gpsimd.memset(w1s_raw[:].bitcast(I32), 0)
         nc.gpsimd.memset(ds_win[:].bitcast(I32), 0)
-        nc.gpsimd.memset(warm_in[:], 0.0)
-        nc.gpsimd.memset(ds_fin[:].bitcast(I32), 0)
-        nc.scalar.activation(warm_out[:], warm_in[:], ACT.Sigmoid)
+        nc.gpsimd.memset(ds[:].bitcast(I32), 0)
 
         nc.sync.dma_start(offs_t[:], offs)
-        for q in range(4):
+        for q in range(QUADRANTS):
             nc.sync.dma_start(xs_win[32 * q : 32 * q + 4, :].bitcast(I32), x_scales[0, 4 * q : 4 * q + 4, :].bitcast(I32))
         nc.sync.dma_start(w1w_raw[:].bitcast(I32), words_of(w1_words))
         nc.sync.dma_start(kq_t[:], kq)
         nc.sync.dma_start(xw_win[:].bitcast(I32), words_of(x_words))
-        for q in range(4):
+        for q in range(QUADRANTS):
             nc.sync.dma_start(w1s_raw[32 * q : 32 * q + 4, :].bitcast(I32), w1_scales[0, 4 * q : 4 * q + 4, :].bitcast(I32))
         nc.sync.dma_start(ds_win[0:P:8, :].bitcast(I32), d_scales[0].bitcast(I32))
         nc.sync.dma_start(r1_t[:], r1)
         nc.sync.dma_start(r2_t[:], r2)
         nc.sync.dma_start(r3_t[:], r3)
         make_identity(nc, ident[:])
+
         y_win = [sb("y_win%d" % t, [P, 2 * S], F32) for t in range(PACK)]
+        y = [y_win[t][:, :S] for t in range(PACK)]
 
         w1w = sb("w1w", [P, PACK, P], U32)
         w1s = sb("w1s", [P, PACK, P], U8)
@@ -90,139 +97,151 @@ def tile_picked_diffevo_none_po_kernel(
         deal_words(w1w, w1w_raw)
         nc.vector.tensor_copy(xs[:], xs_win[:].indirect(offs_t[:]))
         nc.vector.tensor_copy(xw[:], xw_win[:].indirect(offs_t[:]))
-        nc.vector.tensor_copy(w1s[:], w1s_raw[:].rearrange("p (m t) -> p t m", t=PACK))
+        deal_bytes(w1s, w1s_raw)
 
-        gs_t = sb("gs_t", [P, PACK], F32, tag="scales_in")
+        gs_t = sb("gs_t", [P, PACK], F32, tag="w1_scales_then_gs")
         nc.sync.dma_start(gs_t[:], gs.rearrange("(p t) o -> p (t o)", t=PACK))
-        dw_win = sb("dw_win", [P, G], U32, tag="words_in")
-        cr_t = sb("cr_t", [P, S // BLOCK], F32, tag="xs_cr")
-        gs_h = sb("gs_h", [P, PACK], F32)
+        dw_win = sb("dw_win", [P, G], U32, tag="w1_words_then_d_words")
+        cr_t = sb("cr_t", [P, N_BLOCKS], F32, tag="x_scales_then_cr")
+        gs_half = sb("gs_half", [P, PACK], F32)
         with nc.allow_non_contiguous_dma(reason="one value of cr for each partition and block"):
             nc.sync.dma_start(cr_t[:], cr[0:1, :].rearrange("o (c p) -> p (o c)", p=P))
         nc.sync.dma_start(dw_win[:].bitcast(I32), words_of(d_words))
 
-        y_full, y_gs, y_banks = [], [], []
+        y_banks, y_gs = [], []
         for t in range(PACK):
-            bank = ps("y_bank%d" % t, [P, S], t)
+            y_bank = ps("y_bank%d" % t, [P, S], t)
             nc.tensor.matmul_mx(
-                out=bank[:], lhsT=w1w[:, t, :].bitcast(FP8X4), lhsT_scale=w1s[:, t, :],
+                out=y_bank[:], lhsT=w1w[:, t, :].bitcast(FP8X4), lhsT_scale=w1s[:, t, :],
                 rhs=xw[:].bitcast(FP8X4), rhs_scale=xs[:], start=True, stop=True,
             )
-            y_banks.append(bank)
-            y_full.append(y_win[t][:, :S])
+            y_banks.append(y_bank)
             y_gs.append(sb("y_gs%d" % t, [P, S], F32))
-            nc.scalar.copy(y_full[t], bank[:])
-        nc.scalar.activation(gs_h[:], gs_t[:], ACT.Copy, scale=-0.5)
+            nc.scalar.copy(y[t], y_bank[:])
+        nc.scalar.activation(gs_half[:], gs_t[:], ACT.Copy, scale=-0.5)
         for t in range(PACK):
             nc.scalar.activation(y_gs[t][:], y_banks[t][:], ACT.Copy, scale=gs_t[:, t : t + 1])
 
-        ds_g = sb("ds_g", [P, H], U8, tag="xw_in")
-        ds_d = sb("ds_d", [P, PACK, P], U8)
+        ds_picked = sb("ds_picked", [P, H], U8, tag="x_words_then_d_scales")
+        ds_dealt = sb("ds_dealt", [P, PACK, P], U8)
         dw = sb("dw", [P, PACK, P], U32)
-        nc.vector.tensor_copy(ds_g[:], ds_win[:].indirect(kq_t[:]))
-        nc.vector.tensor_copy(ds_d[:], ds_g[:].rearrange("p (m t) -> p t m", t=PACK))
-        ds_flat = ds_d[:].rearrange("p t m -> p (t m)")
+        nc.vector.tensor_copy(ds_picked[:], ds_win[:].indirect(kq_t[:]))
+        deal_bytes(ds_dealt, ds_picked)
+        ds_rows = ds_dealt[:].rearrange("p t m -> p (t m)")
         for r in range(4):
-            nc.sync.dma_start(ds_fin[r:P:32, :].bitcast(I32), ds_flat[8 * r : P : 32, :].bitcast(I32))
+            nc.sync.dma_start(ds[r:P:32, :].bitcast(I32), ds_rows[8 * r : P : 32, :].bitcast(I32))
 
         out_words = sb("out_words", [P, S], U32)
         out_scales = sb("out_scales", [P, S], U8)
         out_rows = out_0.rearrange("(p t) j -> p t j", t=PACK)
 
-        a = [sb("a%d" % t, [P, S], F32) for t in range(PACK)]
-        b = [sb("b%d" % t, [P, S], F32) for t in range(PACK)]
+        sum1 = [sb("sum1_%d" % t, [P, S], F32) for t in range(PACK)]
+        sum2 = [sb("sum2_%d" % t, [P, S], F32) for t in range(PACK)]
         e = [sb("e%d" % t, [P, S], F32) for t in range(PACK)]
-        s = sb("s", [P, PACK, S], F32)
-        tr = sb("tr", [P, PACK, S], F32)
+        gate = sb("gate", [P, PACK, S], F32)
+        tr_gs = sb("tr_gs", [P, PACK, S], F32)
 
         def gather(step, t):
             if step == 0:
-                nc.vector.tensor_scalar(a[t][:], y_win[t][:].indirect(r1_t[:]), 2.0, 0.0, ALU.mult, ALU.add)
+                nc.vector.tensor_scalar(sum1[t][:], y_win[t][:].indirect(r1_t[:]), 2.0, 0.0, ALU.mult, ALU.add)
             elif step == 1:
-                nc.vector.tensor_tensor(b[t][:], y_win[t][:].indirect(r2_t[:]), a[t][:], ALU.add)
+                nc.vector.tensor_tensor(sum2[t][:], y_win[t][:].indirect(r2_t[:]), sum1[t][:], ALU.add)
             else:
-                nc.vector.tensor_tensor(e[t][:], y_win[t][:].indirect(r3_t[:]), b[t][:], ALU.subtract)
+                nc.vector.tensor_tensor(e[t][:], y_win[t][:].indirect(r3_t[:]), sum2[t][:], ALU.subtract)
 
         for wave in range(PACK + 2):
             for step in range(3):
                 if 0 <= wave - step < PACK:
                     gather(step, wave - step)
 
-        dw_g = sb("dw_g", [P, H], U32, tag="b3")
-        nc.vector.tensor_copy(dw_g[:], dw_win[:].indirect(kq_t[:]))
-        deal_words(dw, dw_g)
+        dw_picked = sb("dw_picked", [P, H], U32, tag="sum2_%d" % LAST)
+        nc.vector.tensor_copy(dw_picked[:], dw_win[:].indirect(kq_t[:]))
+        deal_words(dw, dw_picked)
 
-        for t in range(PACK):
-            ut = sb("ut%d" % t, [P, S // BLOCK, P], F32)
-            d_banks = [ps("d_bank%d_%d" % (t, blk), [P, P], 4 + blk) for blk in range(S // BLOCK)]
-            for blk, d_bank in enumerate(d_banks):
-                y_blk = y_full[t][:, blk * BLOCK : (blk + 1) * BLOCK]
-                nc.tensor.matmul(d_bank[:], y_blk, ident[:], start=True, stop=False, is_transpose=True)
-                nc.tensor.matmul(d_bank[:], y_blk, ident[:], start=False, stop=False, is_transpose=True)
-            for blk, d_bank in enumerate(d_banks):
-                nc.tensor.matmul(d_bank[:], e[t][:, blk * BLOCK : (blk + 1) * BLOCK], ident[:], start=False, stop=True, is_transpose=True)
-                nc.scalar.activation(ut[:, blk, :], d_bank[:], ACT.Copy, scale=cr_t[:, blk : blk + 1])
-            u_banks = [ps("u_bank%d" % t, [P, S], t)]
-            if t == PACK - 1:
-                u_banks.append(ps("u_twin", [P, S], 0))
-            for u_bank in u_banks:
-                for blk in range(S // BLOCK):
-                    nc.tensor.transpose(u_bank[:, blk * BLOCK : (blk + 1) * BLOCK], ut[:, blk, :], ident[:])
-            nc.scalar.activation(s[:, t, :], u_banks[0][:], ACT.Sigmoid, scale=-0.5)
-            nc.vector.scalar_tensor_tensor(tr[:, t, :], u_banks[-1][:], gs_h[:, t : t + 1], y_gs[t][:], ALU.mult, ALU.add)
+        def add_turned(acc, values, start, stop):
+            nc.tensor.matmul(acc, values, ident[:], start=start, stop=stop, is_transpose=True)
 
-        def product(acc, t, zw, zs):
-            nc.tensor.matmul_mx(
-                out=acc, lhsT=dw[:, t, :].bitcast(FP8X4), lhsT_scale=ds_fin[:, t * P : (t + 1) * P],
-                rhs=zw.bitcast(FP8X4), rhs_scale=zs, start=True, stop=True,
-            )
+        def turn_back(t, u_turned, blocks, bank):
+            cols = slice(blocks[0] * BLOCK, (blocks[-1] + 1) * BLOCK)
+            u_bank = ps("u_bank%d_%d" % (t, blocks[0]), [P, len(blocks), BLOCK], bank)
+            for i, blk in enumerate(blocks):
+                nc.tensor.transpose(u_bank[:, i, :], u_turned[:, blk, :], ident[:])
+            minus_2u = u_bank[:].rearrange("p b j -> p (b j)")
+            nc.scalar.activation(gate[:, t, cols], minus_2u, ACT.Sigmoid, scale=-0.5)
+            nc.vector.scalar_tensor_tensor(tr_gs[:, t, cols], minus_2u, gs_half[:, t : t + 1], y_gs[t][:, cols], ALU.mult, ALU.add)
 
-        n_blocks = S // BLOCK
-        zb = [sb("zb%d" % blk, [P, BLOCK, PACK], BF16) for blk in range(n_blocks)]
-        zw = [sb("zw%d" % blk, [P, BLOCK], U32) for blk in range(n_blocks)]
-        zs = [sb("zs%d" % blk, [P, BLOCK], U8) for blk in range(n_blocks)]
-        o32 = [sb("o32_%d" % blk, [P, PACK, BLOCK], F32) for blk in range(n_blocks)]
-        ob = sb("ob", [P, S, PACK], BF16)
+        last_banks = [ps("d_last%d" % blk, [P, P], PACK + blk) for blk in range(N_BLOCKS)]
+        for blk in range(N_BLOCKS):
+            add_turned(last_banks[blk][:], y[LAST][:, block(blk)], True, False)
+            add_turned(last_banks[blk][:], y[LAST][:, block(blk)], False, False)
 
-        def gate(blk):
-            cols = slice(blk * BLOCK, (blk + 1) * BLOCK)
+        for t, (sum_bank, back_bank) in enumerate(((0, 1), (2, 3), (0, 2))):
+            u_turned = sb("u_turned%d" % t, [P, N_BLOCKS, P], F32)
+            d_bank = ps("d_bank%d" % t, [P, N_BLOCKS, P], sum_bank)
+            for blk in range(N_BLOCKS):
+                add_turned(d_bank[:, blk, :], y[t][:, block(blk)], True, False)
+                add_turned(d_bank[:, blk, :], y[t][:, block(blk)], False, False)
+                add_turned(d_bank[:, blk, :], e[t][:, block(blk)], False, True)
+            for blk in range(N_BLOCKS):
+                nc.scalar.activation(u_turned[:, blk, :], d_bank[:, blk, :], ACT.Copy, scale=cr_t[:, blk : blk + 1])
+            turn_back(t, u_turned, range(N_BLOCKS), back_bank)
+
+        u_turned = sb("u_turned%d" % LAST, [P, N_BLOCKS, P], F32)
+        for blk in range(N_BLOCKS):
+            add_turned(last_banks[blk][:], e[LAST][:, block(blk)], False, True)
+            nc.scalar.activation(u_turned[:, blk, :], last_banks[blk][:], ACT.Copy, scale=cr_t[:, blk : blk + 1])
+        turn_back(LAST, u_turned, range(0, N_BLOCKS // 2), 0)
+        turn_back(LAST, u_turned, range(N_BLOCKS // 2, N_BLOCKS), PACK)
+
+        z_bf16 = [sb("z_bf16_%d" % blk, [P, BLOCK, PACK], BF16) for blk in range(N_BLOCKS)]
+        zw = [sb("zw%d" % blk, [P, BLOCK], U32) for blk in range(N_BLOCKS)]
+        zs = [sb("zs%d" % blk, [P, BLOCK], U8) for blk in range(N_BLOCKS)]
+        out_f32 = [sb("out_f32_%d" % blk, [P, PACK, BLOCK], F32) for blk in range(N_BLOCKS)]
+        out_bf16 = sb("out_bf16", [P, S, PACK], BF16)
+
+        def from_quarters(ap):
+            return ap.rearrange("p t (c i) -> p c t i", i=2)
+
+        def to_words(ap):
+            return ap.rearrange("p (c i) t -> p c t i", i=2)
+
+        def make_z(blk):
             nc.vector.tensor_tensor(
-                zb[blk][:].rearrange("p (c i) t -> p c t i", i=2),
-                tr[:, :, cols].rearrange("p t (c i) -> p c t i", i=2),
-                s[:, :, cols].rearrange("p t (c i) -> p c t i", i=2),
-                ALU.mult,
+                to_words(z_bf16[blk][:]), from_quarters(tr_gs[:, :, block(blk)]), from_quarters(gate[:, :, block(blk)]), ALU.mult
             )
 
         def multiply(blk):
-            cols = slice(blk * BLOCK, (blk + 1) * BLOCK)
-            nc.vector.quantize_mx(out=zw[blk][:].bitcast(FP8X4), scales=zs[blk][:], in_=zb[blk][:].rearrange("p j t -> p (j t)"))
-            bank = ps("o_bank%d" % blk, [P, PACK, BLOCK], 4 + blk)
+            nc.vector.quantize_mx(
+                out=zw[blk][:].bitcast(FP8X4), scales=zs[blk][:], in_=z_bf16[blk][:].rearrange("p j t -> p (j t)")
+            )
+            out_bank = ps("out_bank%d" % blk, [P, PACK, BLOCK], 7 - blk)
             for t in range(PACK):
-                product(bank[:, t, :], t, zw[blk][:], zs[blk][:])
-            nc.scalar.activation(o32[blk][:], bank[:], ACT.Copy, scale=0.0625)
-            nc.sync.dma_start(out_rows[:, :, cols], o32[blk][:])
+                nc.tensor.matmul_mx(
+                    out=out_bank[:, t, :], lhsT=dw[:, t, :].bitcast(FP8X4), lhsT_scale=ds[:, t * P : (t + 1) * P],
+                    rhs=zw[blk][:].bitcast(FP8X4), rhs_scale=zs[blk][:], start=True, stop=True,
+                )
+            nc.scalar.activation(out_f32[blk][:], out_bank[:], ACT.Copy, scale=OUT_SCALE)
+            nc.sync.dma_start(out_rows[:, :, block(blk)], out_f32[blk][:])
 
         def round_out(blk):
-            nc.vector.tensor_copy(
-                ob[:, blk * BLOCK : (blk + 1) * BLOCK, :].rearrange("p (c i) t -> p c t i", i=2),
-                o32[blk][:].rearrange("p t (c i) -> p c t i", i=2),
-            )
+            nc.vector.tensor_copy(to_words(out_bf16[:, block(blk), :]), from_quarters(out_f32[blk][:]))
 
-        def planes(cols):
+        def quantize_out(cols):
             nc.vector.quantize_mx(
-                out=out_words[:, cols].bitcast(FP8X4), scales=out_scales[:, cols], in_=ob[:, cols, :].rearrange("p j t -> p (j t)")
+                out=out_words[:, cols].bitcast(FP8X4), scales=out_scales[:, cols],
+                in_=out_bf16[:, cols, :].rearrange("p j t -> p (j t)"),
             )
             nc.sync.dma_start(words_of(out_1)[:, cols], out_words[:, cols].bitcast(I32))
 
-        gate(0)
-        for blk in range(1, n_blocks):
-            gate(blk)
+        make_z(0)
+        for blk in range(1, N_BLOCKS):
+            make_z(blk)
             multiply(blk - 1)
-        multiply(n_blocks - 1)
-        for blk in range(n_blocks):
+        multiply(N_BLOCKS - 1)
+        for blk in range(N_BLOCKS):
             round_out(blk)
             if blk % 2:
-                planes(slice((blk - 1) * BLOCK, (blk + 1) * BLOCK))
-        for q in range(4):
-            eng = nc.scalar if q % 2 else nc.sync
-            eng.dma_start(out_2[0, 4 * q : 4 * q + 4, :].bitcast(I32), out_scales[32 * q : 32 * q + 4, :].bitcast(I32))
+                quantize_out(slice((blk - 1) * BLOCK, (blk + 1) * BLOCK))
+        for q in range(QUADRANTS):
+            queue = nc.scalar if q % 2 else nc.sync
+            queue.dma_start(out_2[0, 4 * q : 4 * q + 4, :].bitcast(I32), out_scales[32 * q : 32 * q + 4, :].bitcast(I32))

from contextlib import ExitStack

import concourse.mybir as mybir
from concourse.masks import make_identity

K, T, S, H, G = 512, 2048, 512, 512, 2048
FLOPS = 2 * K * H * S + 2 * H * H * S

F32 = mybir.dt.float32
BF16 = mybir.dt.bfloat16
I32 = mybir.dt.int32
U32 = mybir.dt.uint32
U16 = mybir.dt.uint16
U8 = mybir.dt.uint8
FP8X4 = mybir.dt.float8_e4m3fn_x4
ALU = mybir.AluOpType
ACT = mybir.ActivationFunctionType

P = 128
PACK = 4
QUADRANTS = 4
BLOCK = 128
N_BLOCKS = S // BLOCK
LAST = PACK - 1
OUT_SCALE = 0.0625


def tile_picked_diffevo_none_po_kernel(
    tc, x_words, x_scales, w1_words, w1_scales, cr, gs, d_words, d_scales, offs, r1, r2, r3, kq, out_0, out_1, out_2
):
    nc = tc.nc

    def words_of(dram):
        return dram[0].rearrange("p n t -> p (n t)").bitcast(I32)

    def block(blk):
        return slice(blk * BLOCK, (blk + 1) * BLOCK)

    with ExitStack() as ctx:
        keep = ctx.enter_context(tc.tile_pool(name="keep", bufs=1))
        psum = ctx.enter_context(tc.psum_pool(name="psum", bufs=1))

        def sb(name, shape, dtype, tag=None):
            return keep.tile(shape, dtype, name=name, tag=tag or name, align_bytes=64)

        def ps(name, shape, bank):
            return psum.tile(shape, F32, name=name, tag="bank%d" % bank)

        def deal_words(dealt, plain):
            nc.vector.tensor_copy(
                dealt[:].rearrange("p t (c i) -> p c t i", i=4), plain[:].rearrange("p (c i t) -> p c t i", i=4, t=PACK)
            )

        def deal_bytes(dealt, plain):
            nc.vector.tensor_copy(dealt[:], plain[:].rearrange("p (m t) -> p t m", t=PACK))

        offs_t = sb("offs_t", [P, S // 16], U16)
        r1_t = sb("r1_t", [P, S // 16], U16)
        r2_t = sb("r2_t", [P, S // 16], U16)
        r3_t = sb("r3_t", [P, S // 16], U16)
        kq_t = sb("kq_t", [P, H // 16], U16)

        xs_win = sb("xs_win", [P, T], U8, tag="x_scales_then_cr")
        ds_win = sb("ds_win", [P, G], U8)
        w1s_raw = sb("w1s_raw", [P, H], U8, tag="w1_scales_then_gs")
        ds = sb("ds", [P, H], U8)
        xw_win = sb("xw_win", [P, T], U32, tag="x_words_then_d_scales")
        w1w_raw = sb("w1w_raw", [P, H], U32, tag="w1_words_then_d_words")
        ident = sb("ident", [P, P], F32)

        nc.vector.memset(xs_win[:].bitcast(I32), 0)
        nc.gpsimd.memset(w1s_raw[:].bitcast(I32), 0)
        nc.gpsimd.memset(ds_win[:].bitcast(I32), 0)
        nc.gpsimd.memset(ds[:].bitcast(I32), 0)

        nc.sync.dma_start(offs_t[:], offs)
        for q in range(QUADRANTS):
            nc.sync.dma_start(xs_win[32 * q : 32 * q + 4, :].bitcast(I32), x_scales[0, 4 * q : 4 * q + 4, :].bitcast(I32))
        nc.sync.dma_start(w1w_raw[:].bitcast(I32), words_of(w1_words))
        nc.sync.dma_start(kq_t[:], kq)
        nc.sync.dma_start(xw_win[:].bitcast(I32), words_of(x_words))
        for q in range(QUADRANTS):
            nc.sync.dma_start(w1s_raw[32 * q : 32 * q + 4, :].bitcast(I32), w1_scales[0, 4 * q : 4 * q + 4, :].bitcast(I32))
        nc.sync.dma_start(ds_win[0:P:8, :].bitcast(I32), d_scales[0].bitcast(I32))
        nc.sync.dma_start(r1_t[:], r1)
        nc.sync.dma_start(r2_t[:], r2)
        nc.sync.dma_start(r3_t[:], r3)
        make_identity(nc, ident[:])

        y_win = [sb("y_win%d" % t, [P, 2 * S], F32) for t in range(PACK)]
        y = [y_win[t][:, :S] for t in range(PACK)]

        w1w = sb("w1w", [P, PACK, P], U32)
        w1s = sb("w1s", [P, PACK, P], U8)
        xs = sb("xs", [P, S], U8)
        xw = sb("xw", [P, S], U32)
        deal_words(w1w, w1w_raw)
        nc.vector.tensor_copy(xs[:], xs_win[:].indirect(offs_t[:]))
        nc.vector.tensor_copy(xw[:], xw_win[:].indirect(offs_t[:]))
        deal_bytes(w1s, w1s_raw)

        gs_t = sb("gs_t", [P, PACK], F32, tag="w1_scales_then_gs")
        nc.sync.dma_start(gs_t[:], gs.rearrange("(p t) o -> p (t o)", t=PACK))
        dw_win = sb("dw_win", [P, G], U32, tag="w1_words_then_d_words")
        cr_t = sb("cr_t", [P, N_BLOCKS], F32, tag="x_scales_then_cr")
        gs_half = sb("gs_half", [P, PACK], F32)
        with nc.allow_non_contiguous_dma(reason="one value of cr for each partition and block"):
            nc.sync.dma_start(cr_t[:], cr[0:1, :].rearrange("o (c p) -> p (o c)", p=P))
        nc.sync.dma_start(dw_win[:].bitcast(I32), words_of(d_words))

        y_banks, y_gs = [], []
        for t in range(PACK):
            y_bank = ps("y_bank%d" % t, [P, S], t)
            nc.tensor.matmul_mx(
                out=y_bank[:], lhsT=w1w[:, t, :].bitcast(FP8X4), lhsT_scale=w1s[:, t, :],
                rhs=xw[:].bitcast(FP8X4), rhs_scale=xs[:], start=True, stop=True,
            )
            y_banks.append(y_bank)
            y_gs.append(sb("y_gs%d" % t, [P, S], F32))
            nc.scalar.copy(y[t], y_bank[:])
        nc.scalar.activation(gs_half[:], gs_t[:], ACT.Copy, scale=-0.5)
        for t in range(PACK):
            nc.scalar.activation(y_gs[t][:], y_banks[t][:], ACT.Copy, scale=gs_t[:, t : t + 1])

        ds_picked = sb("ds_picked", [P, H], U8, tag="x_words_then_d_scales")
        ds_dealt = sb("ds_dealt", [P, PACK, P], U8)
        dw = sb("dw", [P, PACK, P], U32)
        nc.vector.tensor_copy(ds_picked[:], ds_win[:].indirect(kq_t[:]))
        deal_bytes(ds_dealt, ds_picked)
        ds_rows = ds_dealt[:].rearrange("p t m -> p (t m)")
        for r in range(4):
            nc.sync.dma_start(ds[r:P:32, :].bitcast(I32), ds_rows[8 * r : P : 32, :].bitcast(I32))

        out_words = sb("out_words", [P, S], U32)
        out_scales = sb("out_scales", [P, S], U8)
        out_rows = out_0.rearrange("(p t) j -> p t j", t=PACK)

        sum1 = [sb("sum1_%d" % t, [P, S], F32) for t in range(PACK)]
        sum2 = [sb("sum2_%d" % t, [P, S], F32) for t in range(PACK)]
        e = [sb("e%d" % t, [P, S], F32) for t in range(PACK)]
        gate = sb("gate", [P, PACK, S], F32)
        tr_gs = sb("tr_gs", [P, PACK, S], F32)

        def gather(step, t):
            if step == 0:
                nc.vector.tensor_scalar(sum1[t][:], y_win[t][:].indirect(r1_t[:]), 2.0, 0.0, ALU.mult, ALU.add)
            elif step == 1:
                nc.vector.tensor_tensor(sum2[t][:], y_win[t][:].indirect(r2_t[:]), sum1[t][:], ALU.add)
            else:
                nc.vector.tensor_tensor(e[t][:], y_win[t][:].indirect(r3_t[:]), sum2[t][:], ALU.subtract)

        for wave in range(PACK + 2):
            for step in range(3):
                if 0 <= wave - step < PACK:
                    gather(step, wave - step)

        dw_picked = sb("dw_picked", [P, H], U32, tag="sum2_%d" % LAST)
        nc.vector.tensor_copy(dw_picked[:], dw_win[:].indirect(kq_t[:]))
        deal_words(dw, dw_picked)

        def add_turned(acc, values, start, stop):
            nc.tensor.matmul(acc, values, ident[:], start=start, stop=stop, is_transpose=True)

        def turn_back(t, u_turned, blocks, bank):
            cols = slice(blocks[0] * BLOCK, (blocks[-1] + 1) * BLOCK)
            u_bank = ps("u_bank%d_%d" % (t, blocks[0]), [P, len(blocks), BLOCK], bank)
            for i, blk in enumerate(blocks):
                nc.tensor.transpose(u_bank[:, i, :], u_turned[:, blk, :], ident[:])
            minus_2u = u_bank[:].rearrange("p b j -> p (b j)")
            nc.scalar.activation(gate[:, t, cols], minus_2u, ACT.Sigmoid, scale=-0.5)
            nc.vector.scalar_tensor_tensor(tr_gs[:, t, cols], minus_2u, gs_half[:, t : t + 1], y_gs[t][:, cols], ALU.mult, ALU.add)

        last_banks = [ps("d_last%d" % blk, [P, P], PACK + blk) for blk in range(N_BLOCKS)]
        for blk in range(N_BLOCKS):
            add_turned(last_banks[blk][:], y[LAST][:, block(blk)], True, False)
            add_turned(last_banks[blk][:], y[LAST][:, block(blk)], False, False)

        for t, (sum_bank, back_bank) in enumerate(((0, 1), (2, 3), (0, 2))):
            u_turned = sb("u_turned%d" % t, [P, N_BLOCKS, P], F32)
            d_bank = ps("d_bank%d" % t, [P, N_BLOCKS, P], sum_bank)
            for blk in range(N_BLOCKS):
                add_turned(d_bank[:, blk, :], y[t][:, block(blk)], True, False)
                add_turned(d_bank[:, blk, :], y[t][:, block(blk)], False, False)
                add_turned(d_bank[:, blk, :], e[t][:, block(blk)], False, True)
            for blk in range(N_BLOCKS):
                nc.scalar.activation(u_turned[:, blk, :], d_bank[:, blk, :], ACT.Copy, scale=cr_t[:, blk : blk + 1])
            turn_back(t, u_turned, range(N_BLOCKS), back_bank)

        u_turned = sb("u_turned%d" % LAST, [P, N_BLOCKS, P], F32)
        for blk in range(N_BLOCKS):
            add_turned(last_banks[blk][:], e[LAST][:, block(blk)], False, True)
            nc.scalar.activation(u_turned[:, blk, :], last_banks[blk][:], ACT.Copy, scale=cr_t[:, blk : blk + 1])
        turn_back(LAST, u_turned, range(0, N_BLOCKS // 2), 0)
        turn_back(LAST, u_turned, range(N_BLOCKS // 2, N_BLOCKS), PACK)

        z_bf16 = [sb("z_bf16_%d" % blk, [P, BLOCK, PACK], BF16) for blk in range(N_BLOCKS)]
        zw = [sb("zw%d" % blk, [P, BLOCK], U32) for blk in range(N_BLOCKS)]
        zs = [sb("zs%d" % blk, [P, BLOCK], U8) for blk in range(N_BLOCKS)]
        out_f32 = [sb("out_f32_%d" % blk, [P, PACK, BLOCK], F32) for blk in range(N_BLOCKS)]
        out_bf16 = sb("out_bf16", [P, S, PACK], BF16)

        def from_quarters(ap):
            return ap.rearrange("p t (c i) -> p c t i", i=2)

        def to_words(ap):
            return ap.rearrange("p (c i) t -> p c t i", i=2)

        def make_z(blk):
            nc.vector.tensor_tensor(
                to_words(z_bf16[blk][:]), from_quarters(tr_gs[:, :, block(blk)]), from_quarters(gate[:, :, block(blk)]), ALU.mult
            )

        def multiply(blk):
            nc.vector.quantize_mx(
                out=zw[blk][:].bitcast(FP8X4), scales=zs[blk][:], in_=z_bf16[blk][:].rearrange("p j t -> p (j t)")
            )
            out_bank = ps("out_bank%d" % blk, [P, PACK, BLOCK], 7 - blk)
            for t in range(PACK):
                nc.tensor.matmul_mx(
                    out=out_bank[:, t, :], lhsT=dw[:, t, :].bitcast(FP8X4), lhsT_scale=ds[:, t * P : (t + 1) * P],
                    rhs=zw[blk][:].bitcast(FP8X4), rhs_scale=zs[blk][:], start=True, stop=True,
                )
            nc.scalar.activation(out_f32[blk][:], out_bank[:], ACT.Copy, scale=OUT_SCALE)
            nc.sync.dma_start(out_rows[:, :, block(blk)], out_f32[blk][:])

        def round_out(blk):
            nc.vector.tensor_copy(to_words(out_bf16[:, block(blk), :]), from_quarters(out_f32[blk][:]))

        def quantize_out(cols):
            nc.vector.quantize_mx(
                out=out_words[:, cols].bitcast(FP8X4), scales=out_scales[:, cols],
                in_=out_bf16[:, cols, :].rearrange("p j t -> p (j t)"),
            )
            nc.sync.dma_start(words_of(out_1)[:, cols], out_words[:, cols].bitcast(I32))

        make_z(0)
        for blk in range(1, N_BLOCKS):
            make_z(blk)
            multiply(blk - 1)
        multiply(N_BLOCKS - 1)
        for blk in range(N_BLOCKS):
            round_out(blk)
            if blk % 2:
                quantize_out(slice((blk - 1) * BLOCK, (blk + 1) * BLOCK))
        for q in range(QUADRANTS):
            queue = nc.scalar if q % 2 else nc.sync
            queue.dma_start(out_2[0, 4 * q : 4 * q + 4, :].bitcast(I32), out_scales[32 * q : 32 * q + 4, :].bitcast(I32))
